import numpy as np
import ml_dtypes


def mxq(x, axis, fmt="e4m3"):
    dtype, down = {"e4m3": (ml_dtypes.float8_e4m3fn, 7), "e5m2": (ml_dtypes.float8_e5m2, 14)}[fmt]
    v = np.moveaxis(np.asarray(x, np.float32).astype(ml_dtypes.bfloat16).astype(np.float64), axis, -1)
    blocks = v.reshape(v.shape[:-1] + (-1, 32))
    amax = np.abs(blocks).max(-1, keepdims=True)
    byte = np.maximum(np.where(amax > 0, np.frexp(amax)[1] - 1 + 127, 0) - down, 1)
    scale = np.exp2(byte - 127.0)
    codes = (blocks / scale).astype(np.float32).astype(dtype).astype(np.float64)
    return np.moveaxis((codes * scale).reshape(v.shape), -1, axis)


WIDE = False


def mx_kscale(k):
    if not WIDE:
        return np.ones(k)
    levels = np.array([10, -10, 5, -5, 0])
    if k % 512:
        return np.exp2(np.random.permutation(np.resize(levels, k // 32))).repeat(32)
    a = np.empty((k // 512, 16))
    for p in range(k // 512):
        a[p, :8] = np.random.permutation(np.resize(levels, 8))
        for g in range(8):
            far = levels[np.abs(levels - a[p, g]) >= 10]
            a[p, g + 8] = far[np.random.randint(len(far))]
    return np.exp2(a.ravel()).repeat(32)


def f64(x):
    return np.asarray(x).astype(np.float64)


def striped8(idx):
    return np.concatenate([v.reshape(-1, 16).T for v in idx]).astype(np.uint16)


def unstriped8(offs):
    return np.stack([offs[16 * g:16 * g + 16].T.reshape(-1) for g in range(8)]).astype(np.int64)


E2M1 = np.array([0.0, 0.5, 1.0, 1.5, 2.0, 3.0, 4.0, 6.0, -0.0, -0.5, -1.0, -1.5, -2.0, -3.0, -4.0, -6.0])


def pack_weight(w, fmt):
    k, n = w.shape
    w = f64(np.asarray(w, np.float32).astype(ml_dtypes.bfloat16)).reshape(k // 32, 32, n)
    amax = np.abs(w).max(1)
    if fmt == "e4m3":
        byte = np.frexp(amax)[1] - 1 + 127 - 7
    else:
        mant, ex = np.frexp(amax / 6.0)
        byte = np.where(mant > 0.5, ex, ex - 1) + 127
    byte = np.clip(np.where(amax > 0, byte, 1), 1, 254)
    scaled = (w * np.exp2(127.0 - byte)[:, None, :]).reshape(k, n).astype(np.float32)
    by_word = np.ascontiguousarray(scaled.reshape(k // 512, 128, 4, n).transpose(0, 1, 3, 2))
    if fmt == "e4m3":
        words = by_word.astype(ml_dtypes.float8_e4m3fn).view(np.uint8)
    else:
        c = by_word.astype(ml_dtypes.float4_e2m1fn).view(np.uint8) & 0xF
        words = (c[..., 0::2] | (c[..., 1::2] << 4)).reshape(k // 512, 128, 2 * n)
    return np.ascontiguousarray(words), np.ascontiguousarray(byte.astype(np.uint8).reshape(k // 512, 16, n))


def unpack_weight(words, scales, fmt):
    g, _, n = scales.shape
    words = np.ascontiguousarray(words).reshape(g, 128, n, -1)
    if fmt == "e4m3":
        vals = words.view(ml_dtypes.float8_e4m3fn).astype(np.float64)
    else:
        nib = np.empty((g, 128, n, 4), np.uint8)
        nib[..., 0::2] = words & 0xF
        nib[..., 1::2] = words >> 4
        vals = E2M1[nib]
    vals = vals * np.repeat(np.exp2(scales.astype(np.float64) - 127.0), 8, axis=1)[..., None]
    return vals.transpose(0, 1, 3, 2).reshape(g * 512, n)


def silu(v):
    return v / (1.0 + np.exp(-np.maximum(v, -700.0)))


K, M, T, S = 512, 128, 2048, 1024


def setup_inputs():
    n = np.random.standard_normal
    s = mx_kscale(K)[:, None]
    p_w4 = pack_weight(n((K, M)) / np.sqrt(K) / s, "e2m1")
    return {
        "xT": (n((K, T)) * s).astype(np.float32),
        "w4_words": p_w4[0],
        "w4_scales": p_w4[1],
        "w8": (n((K, M)) / np.sqrt(K) / s).astype(np.float32),
        "wgt": np.repeat(np.random.uniform(0.5, 2.0, (8, S)), 16, axis=0).astype(np.float32),
        "offs": striped8(np.stack([np.random.permutation(T)[:S] for _ in range(8)])),
    }


def reference(xT, w4_words, w4_scales, w8, wgt, offs):
    idx = unstriped8(offs)
    group = np.arange(K) % 512 // 64
    xg = f64(wgt)[np.arange(K) // 4 % 128] * f64(xT)[np.arange(K)[:, None], idx[group]]
    xT_ = mxq(xg, 0, "e4m3")
    w4_ = unpack_weight(w4_words, w4_scales, "e2m1")
    w8_ = mxq(f64(w8), 0, "e4m3")
    y = w4_.T @ xT_
    u = w8_.T @ xT_
    y = silu(y) * u
    return y

@@ -1,0 +1,125 @@
+from contextlib import ExitStack
+
+import concourse.mybir as mybir
+
+K, M, T, S = 512, 128, 2048, 1024
+FLOPS = 2 * 2 * K * M * S
+
+F32 = mybir.dt.float32
+BF16 = mybir.dt.bfloat16
+I32 = mybir.dt.int32
+U32 = mybir.dt.uint32
+U16 = mybir.dt.uint16
+U8 = mybir.dt.uint8
+FP8X4 = mybir.dt.float8_e4m3fn_x4
+FP4X4 = mybir.dt.float4_e2m1fn_x4
+MULT = mybir.AluOpType.mult
+SILU = mybir.ActivationFunctionType.Silu
+
+P = 128
+PACK = 4
+GROUP = 16
+CHUNKS = (128, 256, 256, 256, 128)
+SPLIT = CHUNKS[0] + CHUNKS[1]
+PARTS = ((0, SPLIT), (SPLIT, S))
+
+
+def tile_list_hglu_none_kernel(tc, xT, w4_words, w4_scales, w8, wgt, offs, out):
+    nc = tc.nc
+    starts = [sum(CHUNKS[:c]) for c in range(len(CHUNKS))]
+    with ExitStack() as ctx:
+        keep = ctx.enter_context(tc.tile_pool(name="keep", bufs=1))
+        psum = ctx.enter_context(tc.psum_pool(name="psum", bufs=1))
+
+        offsets = keep.tile([P, S // GROUP], U16, name="offsets")
+        planes = [keep.tile([P, T], F32, name=f"plane{i}") for i in range(PACK)]
+        wgt_part = [keep.tile([P, b - a], F32, name=f"wgt{h}") for h, (a, b) in enumerate(PARTS)]
+        w8_raw = keep.tile([P, PACK, M], F32, name="w8_raw")
+        w8_bf = keep.tile([P, M, PACK], BF16, name="w8_bf", align_bytes=64)
+        w8_codes = keep.tile([P, M], U32, name="w8_codes", align_bytes=64)
+        w8_sc = keep.tile([P, M], U8, name="w8_sc", align_bytes=64)
+        w4_codes = keep.tile([P, 2 * M], U8, name="w4_codes", align_bytes=64)
+        w4_sc = keep.tile([P, M], U8, name="w4_sc", align_bytes=64)
+        warm_in = keep.tile([P, 1], F32, name="warm_in")
+        warm_out = keep.tile([P, 1], F32, name="warm_out")
+
+        x_planes = xT.rearrange("(p i) t -> i p t", i=PACK)
+
+        nc.vector.memset(warm_in[:], 0.0)
+        nc.scalar.activation(warm_out[:], warm_in[:], SILU)
+        nc.vector.memset(w4_sc[:].bitcast(U32), 0)
+
+        nc.sync.dma_start(planes[0][:], x_planes[0])
+        nc.sync.dma_start(offsets[:], offs)
+        for h, (a, b) in enumerate(PARTS):
+            nc.sync.dma_start(wgt_part[h][:], wgt[:, a:b])
+        nc.sync.dma_start(w8_raw[:], w8.rearrange("(p i) n -> p i n", i=PACK))
+        nc.sync.dma_start(planes[1][:], x_planes[1])
+        nc.sync.dma_start(planes[2][:], x_planes[2])
+        nc.sync.dma_start(planes[3][:], x_planes[3])
+        nc.sync.dma_start(w4_codes[:].bitcast(I32), w4_words[0].bitcast(I32))
+        for q in range(4):
+            nc.sync.dma_start(w4_sc[32 * q : 32 * q + 4, :].bitcast(I32), w4_scales[0, 4 * q : 4 * q + 4, :].bitcast(I32))
+
+        def gather(dst, i, j0, width):
+            h = int(j0 >= SPLIT)
+            j = j0 - PARTS[h][0]
+            nc.vector.tensor_tensor(
+                dst,
+                planes[i][:].indirect(offsets[:, j0 // GROUP : (j0 + width) // GROUP]),
+                wgt_part[h][:, j : j + width],
+                MULT,
+            )
+
+        low = [keep.tile([P, 2, b - a], F32, name=f"low{h}") for h, (a, b) in enumerate(PARTS)]
+        high = [keep.tile([P, 2, w], F32, name=f"high{c}") for c, w in enumerate(CHUNKS)]
+        xg_bf = [keep.tile([P, w, PACK], BF16, name=f"xg_bf{c}", align_bytes=64) for c, w in enumerate(CHUNKS)]
+        xg_codes = [keep.tile([P, w], U32, name=f"xg_codes{c}", align_bytes=64) for c, w in enumerate(CHUNKS)]
+        xg_sc = [keep.tile([P, w], U8, name=f"xg_sc{c}", align_bytes=64) for c, w in enumerate(CHUNKS)]
+        gate = [keep.tile([P, w], F32, name=f"gate{c}") for c, w in enumerate(CHUNKS)]
+        result = [keep.tile([P, w], F32, name=f"result{c}") for c, w in enumerate(CHUNKS)]
+
+        for h, (a, b) in enumerate(PARTS):
+            gather(low[h][:, 0, :], 0, a, b - a)
+        nc.scalar.copy(w8_bf[:], w8_raw[:].rearrange("p i n -> p n i"))
+        nc.vector.quantize_mx(out=w8_codes[:].bitcast(FP8X4), scales=w8_sc[:], in_=w8_bf[:].rearrange("p n i -> p (n i)"))
+
+        for h, (a, b) in enumerate(PARTS):
+            gather(low[h][:, 1, :], 1, a, b - a)
+        for c, w in enumerate(CHUNKS):
+            h = int(starts[c] >= SPLIT)
+            j = starts[c] - PARTS[h][0]
+            nc.scalar.copy(xg_bf[c][:, :, 0:2], low[h][:, :, j : j + w].rearrange("p i j -> p j i"))
+
+        for c, w in enumerate(CHUNKS):
+            gather(high[c][:, 0, :], 2, starts[c], w)
+
+        for c, w in enumerate(CHUNKS):
+            gather(high[c][:, 1, :], 3, starts[c], w)
+        for c, w in enumerate(CHUNKS):
+            nc.scalar.copy(xg_bf[c][:, :, 2:4], high[c][:].rearrange("p i j -> p j i"))
+        sums = []
+        for c, w in enumerate(CHUNKS):
+            nc.vector.quantize_mx(
+                out=xg_codes[c][:].bitcast(FP8X4), scales=xg_sc[c][:], in_=xg_bf[c][:].rearrange("p j i -> p (j i)")
+            )
+            if c < 2:
+                both = psum.tile([P, 2, w], F32, name=f"both{c}")
+                e_ps, u_ps = both[:, 0, :], both[:, 1, :]
+            else:
+                e_ps = psum.tile([P, w], F32, name=f"e_ps{c}")[:]
+                u_ps = psum.tile([P, w], F32, name=f"u_ps{c}")[:]
+            nc.tensor.matmul_mx(
+                out=e_ps, lhsT=w4_codes[:].bitcast(FP4X4), lhsT_scale=w4_sc[:],
+                rhs=xg_codes[c][:].bitcast(FP8X4), rhs_scale=xg_sc[c][:], start=True, stop=True,
+            )
+            nc.tensor.matmul_mx(
+                out=u_ps, lhsT=w8_codes[:].bitcast(FP8X4), lhsT_scale=w8_sc[:],
+                rhs=xg_codes[c][:].bitcast(FP8X4), rhs_scale=xg_sc[c][:], start=True, stop=True,
+            )
+            sums.append((e_ps, u_ps))
+        for c, w in enumerate(CHUNKS):
+            e_ps, u_ps = sums[c]
+            nc.scalar.activation(gate[c][:], e_ps, SILU)
+            nc.vector.tensor_tensor(result[c][:], u_ps, gate[c][:], MULT)
+            nc.sync.dma_start(out[:, starts[c] : starts[c] + w], result[c][:])

@@ -19,8 +19,9 @@ SILU = mybir.ActivationFunctionType.Silu
 P = 128
 PACK = 4
 GROUP = 16
-CHUNKS = (128, 256, 256, 256, 128)
-SPLIT = CHUNKS[0] + CHUNKS[1]
+CHUNKS = (256, 256, 256, 128, 128)
+AHEAD = 3
+SPLIT = S // 2
 PARTS = ((0, SPLIT), (SPLIT, S))
 
 
@@ -29,6 +30,7 @@ def tile_list_hglu_none_kernel(tc, xT, w4_words, w4_scales, w8, wgt, offs, out):
     starts = [sum(CHUNKS[:c]) for c in range(len(CHUNKS))]
     with ExitStack() as ctx:
         keep = ctx.enter_context(tc.tile_pool(name="keep", bufs=1))
+        ring = ctx.enter_context(tc.tile_pool(name="ring", bufs=AHEAD))
         psum = ctx.enter_context(tc.psum_pool(name="psum", bufs=1))
 
         offsets = keep.tile([P, S // GROUP], U16, name="offsets")
@@ -47,19 +49,20 @@ def tile_list_hglu_none_kernel(tc, xT, w4_words, w4_scales, w8, wgt, offs, out):
 
         nc.vector.memset(warm_in[:], 0.0)
         nc.scalar.activation(warm_out[:], warm_in[:], SILU)
-        nc.vector.memset(w4_sc[:].bitcast(U32), 0)
+        nc.gpsimd.memset(w4_sc[:].bitcast(U32), 0)
+        nc.gpsimd.dma_start(w4_codes[:].bitcast(I32), w4_words[0].bitcast(I32))
+        for q in range(4):
+            nc.gpsimd.dma_start(w4_sc[32 * q : 32 * q + 4, :].bitcast(I32), w4_scales[0, 4 * q : 4 * q + 4, :].bitcast(I32))
+
 
         nc.sync.dma_start(planes[0][:], x_planes[0])
         nc.sync.dma_start(offsets[:], offs)
         for h, (a, b) in enumerate(PARTS):
             nc.sync.dma_start(wgt_part[h][:], wgt[:, a:b])
-        nc.sync.dma_start(w8_raw[:], w8.rearrange("(p i) n -> p i n", i=PACK))
         nc.sync.dma_start(planes[1][:], x_planes[1])
+        nc.sync.dma_start(w8_raw[:], w8.rearrange("(p i) n -> p i n", i=PACK))
         nc.sync.dma_start(planes[2][:], x_planes[2])
         nc.sync.dma_start(planes[3][:], x_planes[3])
-        nc.sync.dma_start(w4_codes[:].bitcast(I32), w4_words[0].bitcast(I32))
-        for q in range(4):
-            nc.sync.dma_start(w4_sc[32 * q : 32 * q + 4, :].bitcast(I32), w4_scales[0, 4 * q : 4 * q + 4, :].bitcast(I32))
 
         def gather(dst, i, j0, width):
             h = int(j0 >= SPLIT)
@@ -72,34 +75,35 @@ def tile_list_hglu_none_kernel(tc, xT, w4_words, w4_scales, w8, wgt, offs, out):
             )
 
         low = [keep.tile([P, 2, b - a], F32, name=f"low{h}") for h, (a, b) in enumerate(PARTS)]
-        high = [keep.tile([P, 2, w], F32, name=f"high{c}") for c, w in enumerate(CHUNKS)]
         xg_bf = [keep.tile([P, w, PACK], BF16, name=f"xg_bf{c}", align_bytes=64) for c, w in enumerate(CHUNKS)]
         xg_codes = [keep.tile([P, w], U32, name=f"xg_codes{c}", align_bytes=64) for c, w in enumerate(CHUNKS)]
         xg_sc = [keep.tile([P, w], U8, name=f"xg_sc{c}", align_bytes=64) for c, w in enumerate(CHUNKS)]
         gate = [keep.tile([P, w], F32, name=f"gate{c}") for c, w in enumerate(CHUNKS)]
         result = [keep.tile([P, w], F32, name=f"result{c}") for c, w in enumerate(CHUNKS)]
 
-        for h, (a, b) in enumerate(PARTS):
-            gather(low[h][:, 0, :], 0, a, b - a)
+        for i in range(2):
+            for h, (a, b) in enumerate(PARTS):
+                gather(low[h][:, i, :], i, a, b - a)
         nc.scalar.copy(w8_bf[:], w8_raw[:].rearrange("p i n -> p n i"))
-        nc.vector.quantize_mx(out=w8_codes[:].bitcast(FP8X4), scales=w8_sc[:], in_=w8_bf[:].rearrange("p n i -> p (n i)"))
-
-        for h, (a, b) in enumerate(PARTS):
-            gather(low[h][:, 1, :], 1, a, b - a)
         for c, w in enumerate(CHUNKS):
             h = int(starts[c] >= SPLIT)
             j = starts[c] - PARTS[h][0]
             nc.scalar.copy(xg_bf[c][:, :, 0:2], low[h][:, :, j : j + w].rearrange("p i j -> p j i"))
+        nc.vector.quantize_mx(out=w8_codes[:].bitcast(FP8X4), scales=w8_sc[:], in_=w8_bf[:].rearrange("p n i -> p (n i)"))
 
-        for c, w in enumerate(CHUNKS):
-            gather(high[c][:, 0, :], 2, starts[c], w)
-
-        for c, w in enumerate(CHUNKS):
-            gather(high[c][:, 1, :], 3, starts[c], w)
-        for c, w in enumerate(CHUNKS):
-            nc.scalar.copy(xg_bf[c][:, :, 2:4], high[c][:].rearrange("p i j -> p j i"))
+        high = []
         sums = []
-        for c, w in enumerate(CHUNKS):
+
+        def pick_third(c):
+            high.append(ring.tile([P, 2, CHUNKS[c]], F32, name="high"))
+            gather(high[c][:, 0, :], 2, starts[c], CHUNKS[c])
+
+        def pick_fourth(c):
+            gather(high[c][:, 1, :], 3, starts[c], CHUNKS[c])
+            nc.scalar.copy(xg_bf[c][:, :, 2:4], high[c][:].rearrange("p i j -> p j i"))
+
+        def multiply(c):
+            w = CHUNKS[c]
             nc.vector.quantize_mx(
                 out=xg_codes[c][:].bitcast(FP8X4), scales=xg_sc[c][:], in_=xg_bf[c][:].rearrange("p j i -> p (j i)")
             )
@@ -118,8 +122,23 @@ def tile_list_hglu_none_kernel(tc, xT, w4_words, w4_scales, w8, wgt, offs, out):
                 rhs=xg_codes[c][:].bitcast(FP8X4), rhs_scale=xg_sc[c][:], start=True, stop=True,
             )
             sums.append((e_ps, u_ps))
-        for c, w in enumerate(CHUNKS):
+
+        def finish(c):
             e_ps, u_ps = sums[c]
             nc.scalar.activation(gate[c][:], e_ps, SILU)
             nc.vector.tensor_tensor(result[c][:], u_ps, gate[c][:], MULT)
-            nc.sync.dma_start(out[:, starts[c] : starts[c] + w], result[c][:])
+            nc.sync.dma_start(out[:, starts[c] : starts[c] + CHUNKS[c]], result[c][:])
+
+        for c in range(AHEAD):
+            pick_third(c)
+        for c in range(AHEAD):
+            pick_fourth(c)
+        for c in range(len(CHUNKS)):
+            multiply(c)
+            if c + AHEAD < len(CHUNKS):
+                pick_third(c + AHEAD)
+                pick_fourth(c + AHEAD)
+            if c >= 2:
+                finish(c - 2)
+        for c in range(len(CHUNKS) - 2, len(CHUNKS)):
+            finish(c)

@@ -1,6 +1,7 @@
 from contextlib import ExitStack
 
 import concourse.mybir as mybir
+from concourse.masks import make_identity
 
 K, M, T, S = 512, 128, 2048, 1024
 FLOPS = 2 * 2 * K * M * S
@@ -37,7 +38,6 @@ def tile_list_hglu_none_kernel(tc, xT, w4_words, w4_scales, w8, wgt, offs, out):
         planes = [keep.tile([P, T], F32, name=f"plane{i}") for i in range(PACK)]
         wgt_part = [keep.tile([P, b - a], F32, name=f"wgt{h}") for h, (a, b) in enumerate(PARTS)]
         w8_raw = keep.tile([P, PACK, M], F32, name="w8_raw")
-        w8_bf = keep.tile([P, M, PACK], BF16, name="w8_bf", align_bytes=64)
         w8_codes = keep.tile([P, M], U32, name="w8_codes", align_bytes=64)
         w8_sc = keep.tile([P, M], U8, name="w8_sc", align_bytes=64)
         w4_codes = keep.tile([P, 2 * M], U8, name="w4_codes", align_bytes=64)
@@ -49,20 +49,38 @@ def tile_list_hglu_none_kernel(tc, xT, w4_words, w4_scales, w8, wgt, offs, out):
 
         nc.vector.memset(warm_in[:], 0.0)
         nc.scalar.activation(warm_out[:], warm_in[:], SILU)
-        nc.gpsimd.memset(w4_sc[:].bitcast(U32), 0)
+        identity = keep.tile([P, P], F32, name="identity")
+        make_identity(nc, identity[:])
+        nc.vector.memset(w4_sc[:].bitcast(U32), 0)
         nc.gpsimd.dma_start(w4_codes[:].bitcast(I32), w4_words[0].bitcast(I32))
         for q in range(4):
             nc.gpsimd.dma_start(w4_sc[32 * q : 32 * q + 4, :].bitcast(I32), w4_scales[0, 4 * q : 4 * q + 4, :].bitcast(I32))
 
 
+        wgt_rows = keep.tile([P, P], F32, name="wgt_rows")
+        nc.vector.memset(wgt_rows[64:128, :], 0.0)
+        nc.sync.dma_start(wgt_rows[0:64, :], wgt.rearrange("(g s) (r c) -> s g r c", s=GROUP, c=P)[0])
         nc.sync.dma_start(planes[0][:], x_planes[0])
         nc.sync.dma_start(offsets[:], offs)
-        for h, (a, b) in enumerate(PARTS):
-            nc.sync.dma_start(wgt_part[h][:], wgt[:, a:b])
         nc.sync.dma_start(planes[1][:], x_planes[1])
         nc.sync.dma_start(w8_raw[:], w8.rearrange("(p i) n -> p i n", i=PACK))
         nc.sync.dma_start(planes[2][:], x_planes[2])
         nc.sync.dma_start(planes[3][:], x_planes[3])
+
+        copies = (nc.vector.tensor_copy, nc.scalar.copy)
+        turned = [psum.tile([P, P], F32, name=f"turned{h}", tag=f"bank{h}") for h in range(2)]
+        for h in range(2):
+            nc.tensor.transpose(turned[h][:], wgt_rows[:], identity[:])
+        for h in range(2):
+            for quarter in range(2):
+                r0 = 4 * h + 2 * quarter
+                spread = keep.tile([P, 2, 8, GROUP], F32, name=f"spread{h}{quarter}", align_bytes=64)
+                src = turned[h][:, 0:64].rearrange("c (g r) -> c r g", r=8)[:, r0 : r0 + 2, :]
+                copies[h](spread[:], src.unsqueeze(3).to_broadcast([P, 2, 8, GROUP]))
+                back = psum.tile([P, 2, P], F32, name=f"back{h}{quarter}", tag=f"bank{2 + 2 * h + quarter}")
+                for r in range(2):
+                    nc.tensor.transpose(back[:, r, :], spread[:, r].rearrange("c g s -> c (g s)"), identity[:])
+                copies[h](wgt_part[h][:, 256 * quarter : 256 * (quarter + 1)], back[:].rearrange("p r c -> p (r c)"))
 
         def gather(dst, i, j0, width):
             h = int(j0 >= SPLIT)
@@ -84,6 +102,7 @@ def tile_list_hglu_none_kernel(tc, xT, w4_words, w4_scales, w8, wgt, offs, out):
         for i in range(2):
             for h, (a, b) in enumerate(PARTS):
                 gather(low[h][:, i, :], i, a, b - a)
+        w8_bf = keep.tile([P, M, PACK], BF16, name="w8_bf", tag="spread11", align_bytes=64)
         nc.scalar.copy(w8_bf[:], w8_raw[:].rearrange("p i n -> p n i"))
         for c, w in enumerate(CHUNKS):
             h = int(starts[c] >= SPLIT)
@@ -108,11 +127,11 @@ def tile_list_hglu_none_kernel(tc, xT, w4_words, w4_scales, w8, wgt, offs, out):
                 out=xg_codes[c][:].bitcast(FP8X4), scales=xg_sc[c][:], in_=xg_bf[c][:].rearrange("p j i -> p (j i)")
             )
             if c < 2:
-                both = psum.tile([P, 2, w], F32, name=f"both{c}")
+                both = psum.tile([P, 2, w], F32, name=f"both{c}", tag=f"bank{c}")
                 e_ps, u_ps = both[:, 0, :], both[:, 1, :]
             else:
-                e_ps = psum.tile([P, w], F32, name=f"e_ps{c}")[:]
-                u_ps = psum.tile([P, w], F32, name=f"u_ps{c}")[:]
+                e_ps = psum.tile([P, w], F32, name=f"e_ps{c}", tag=f"bank{2 * c - 2}")[:]
+                u_ps = psum.tile([P, w], F32, name=f"u_ps{c}", tag=f"bank{2 * c - 1}")[:]
             nc.tensor.matmul_mx(
                 out=e_ps, lhsT=w4_codes[:].bitcast(FP4X4), lhsT_scale=w4_sc[:],
                 rhs=xg_codes[c][:].bitcast(FP8X4), rhs_scale=xg_sc[c][:], start=True, stop=True,
@@ -133,12 +152,15 @@ def tile_list_hglu_none_kernel(tc, xT, w4_words, w4_scales, w8, wgt, offs, out):
             pick_third(c)
         for c in range(AHEAD):
             pick_fourth(c)
-        for c in range(len(CHUNKS)):
-            multiply(c)
-            if c + AHEAD < len(CHUNKS):
-                pick_third(c + AHEAD)
-                pick_fourth(c + AHEAD)
-            if c >= 2:
-                finish(c - 2)
-        for c in range(len(CHUNKS) - 2, len(CHUNKS)):
+        multiply(0)
+        pick_third(3)
+        pick_fourth(3)
+        multiply(1)
+        pick_third(4)
+        multiply(2)
+        pick_fourth(4)
+        finish(0)
+        multiply(3)
+        multiply(4)
+        for c in range(1, len(CHUNKS)):
             finish(c)

from contextlib import ExitStack

import concourse.mybir as mybir
from concourse.masks import make_identity

K, M, T, S = 512, 128, 2048, 1024
FLOPS = 2 * 2 * K * M * S

F32 = mybir.dt.float32
BF16 = mybir.dt.bfloat16
I32 = mybir.dt.int32
U32 = mybir.dt.uint32
U16 = mybir.dt.uint16
U8 = mybir.dt.uint8
FP8X4 = mybir.dt.float8_e4m3fn_x4
FP4X4 = mybir.dt.float4_e2m1fn_x4
MULT = mybir.AluOpType.mult
SILU = mybir.ActivationFunctionType.Silu

P = 128
PACK = 4
GROUP = 16
CHUNKS = (256, 256, 256, 128, 128)
AHEAD = 3
SPLIT = S // 2
PARTS = ((0, SPLIT), (SPLIT, S))


def tile_list_hglu_none_kernel(tc, xT, w4_words, w4_scales, w8, wgt, offs, out):
    nc = tc.nc
    starts = [sum(CHUNKS[:c]) for c in range(len(CHUNKS))]
    with ExitStack() as ctx:
        keep = ctx.enter_context(tc.tile_pool(name="keep", bufs=1))
        ring = ctx.enter_context(tc.tile_pool(name="ring", bufs=AHEAD))
        psum = ctx.enter_context(tc.psum_pool(name="psum", bufs=1))

        offsets = keep.tile([P, S // GROUP], U16, name="offsets")
        planes = [keep.tile([P, T], F32, name=f"plane{i}") for i in range(PACK)]
        wgt_part = [keep.tile([P, b - a], F32, name=f"wgt{h}") for h, (a, b) in enumerate(PARTS)]
        w8_raw = keep.tile([P, PACK, M], F32, name="w8_raw")
        w8_codes = keep.tile([P, M], U32, name="w8_codes", align_bytes=64)
        w8_sc = keep.tile([P, M], U8, name="w8_sc", align_bytes=64)
        w4_codes = keep.tile([P, 2 * M], U8, name="w4_codes", align_bytes=64)
        w4_sc = keep.tile([P, M], U8, name="w4_sc", align_bytes=64)
        warm_in = keep.tile([P, 1], F32, name="warm_in")
        warm_out = keep.tile([P, 1], F32, name="warm_out")

        x_planes = xT.rearrange("(p i) t -> i p t", i=PACK)

        nc.vector.memset(warm_in[:], 0.0)
        nc.scalar.activation(warm_out[:], warm_in[:], SILU)
        identity = keep.tile([P, P], F32, name="identity")
        make_identity(nc, identity[:])
        nc.vector.memset(w4_sc[:].bitcast(U32), 0)
        nc.gpsimd.dma_start(w4_codes[:].bitcast(I32), w4_words[0].bitcast(I32))
        for q in range(4):
            nc.gpsimd.dma_start(w4_sc[32 * q : 32 * q + 4, :].bitcast(I32), w4_scales[0, 4 * q : 4 * q + 4, :].bitcast(I32))


        wgt_rows = keep.tile([P, P], F32, name="wgt_rows")
        nc.vector.memset(wgt_rows[64:128, :], 0.0)
        nc.sync.dma_start(wgt_rows[0:64, :], wgt.rearrange("(g s) (r c) -> s g r c", s=GROUP, c=P)[0])
        nc.sync.dma_start(planes[0][:], x_planes[0])
        nc.sync.dma_start(offsets[:], offs)
        nc.sync.dma_start(planes[1][:], x_planes[1])
        nc.sync.dma_start(w8_raw[:], w8.rearrange("(p i) n -> p i n", i=PACK))
        nc.sync.dma_start(planes[2][:], x_planes[2])
        nc.sync.dma_start(planes[3][:], x_planes[3])

        copies = (nc.vector.tensor_copy, nc.scalar.copy)
        turned = [psum.tile([P, P], F32, name=f"turned{h}", tag=f"bank{h}") for h in range(2)]
        for h in range(2):
            nc.tensor.transpose(turned[h][:], wgt_rows[:], identity[:])
        for h in range(2):
            for quarter in range(2):
                r0 = 4 * h + 2 * quarter
                spread = keep.tile([P, 2, 8, GROUP], F32, name=f"spread{h}{quarter}", align_bytes=64)
                src = turned[h][:, 0:64].rearrange("c (g r) -> c r g", r=8)[:, r0 : r0 + 2, :]
                copies[h](spread[:], src.unsqueeze(3).to_broadcast([P, 2, 8, GROUP]))
                back = psum.tile([P, 2, P], F32, name=f"back{h}{quarter}", tag=f"bank{2 + 2 * h + quarter}")
                for r in range(2):
                    nc.tensor.transpose(back[:, r, :], spread[:, r].rearrange("c g s -> c (g s)"), identity[:])
                copies[h](wgt_part[h][:, 256 * quarter : 256 * (quarter + 1)], back[:].rearrange("p r c -> p (r c)"))

        def gather(dst, i, j0, width):
            h = int(j0 >= SPLIT)
            j = j0 - PARTS[h][0]
            nc.vector.tensor_tensor(
                dst,
                planes[i][:].indirect(offsets[:, j0 // GROUP : (j0 + width) // GROUP]),
                wgt_part[h][:, j : j + width],
                MULT,
            )

        low = [keep.tile([P, 2, b - a], F32, name=f"low{h}") for h, (a, b) in enumerate(PARTS)]
        xg_bf = [keep.tile([P, w, PACK], BF16, name=f"xg_bf{c}", align_bytes=64) for c, w in enumerate(CHUNKS)]
        xg_codes = [keep.tile([P, w], U32, name=f"xg_codes{c}", align_bytes=64) for c, w in enumerate(CHUNKS)]
        xg_sc = [keep.tile([P, w], U8, name=f"xg_sc{c}", align_bytes=64) for c, w in enumerate(CHUNKS)]
        gate = [keep.tile([P, w], F32, name=f"gate{c}") for c, w in enumerate(CHUNKS)]
        result = [keep.tile([P, w], F32, name=f"result{c}") for c, w in enumerate(CHUNKS)]

        for i in range(2):
            for h, (a, b) in enumerate(PARTS):
                gather(low[h][:, i, :], i, a, b - a)
        w8_bf = keep.tile([P, M, PACK], BF16, name="w8_bf", tag="spread11", align_bytes=64)
        nc.scalar.copy(w8_bf[:], w8_raw[:].rearrange("p i n -> p n i"))
        for c, w in enumerate(CHUNKS):
            h = int(starts[c] >= SPLIT)
            j = starts[c] - PARTS[h][0]
            nc.scalar.copy(xg_bf[c][:, :, 0:2], low[h][:, :, j : j + w].rearrange("p i j -> p j i"))
        nc.vector.quantize_mx(out=w8_codes[:].bitcast(FP8X4), scales=w8_sc[:], in_=w8_bf[:].rearrange("p n i -> p (n i)"))

        high = []
        sums = []

        def pick_third(c):
            high.append(ring.tile([P, 2, CHUNKS[c]], F32, name="high"))
            gather(high[c][:, 0, :], 2, starts[c], CHUNKS[c])

        def pick_fourth(c):
            gather(high[c][:, 1, :], 3, starts[c], CHUNKS[c])
            nc.scalar.copy(xg_bf[c][:, :, 2:4], high[c][:].rearrange("p i j -> p j i"))

        def multiply(c):
            w = CHUNKS[c]
            nc.vector.quantize_mx(
                out=xg_codes[c][:].bitcast(FP8X4), scales=xg_sc[c][:], in_=xg_bf[c][:].rearrange("p j i -> p (j i)")
            )
            if c < 2:
                both = psum.tile([P, 2, w], F32, name=f"both{c}", tag=f"bank{c}")
                e_ps, u_ps = both[:, 0, :], both[:, 1, :]
            else:
                e_ps = psum.tile([P, w], F32, name=f"e_ps{c}", tag=f"bank{2 * c - 2}")[:]
                u_ps = psum.tile([P, w], F32, name=f"u_ps{c}", tag=f"bank{2 * c - 1}")[:]
            nc.tensor.matmul_mx(
                out=e_ps, lhsT=w4_codes[:].bitcast(FP4X4), lhsT_scale=w4_sc[:],
                rhs=xg_codes[c][:].bitcast(FP8X4), rhs_scale=xg_sc[c][:], start=True, stop=True,
            )
            nc.tensor.matmul_mx(
                out=u_ps, lhsT=w8_codes[:].bitcast(FP8X4), lhsT_scale=w8_sc[:],
                rhs=xg_codes[c][:].bitcast(FP8X4), rhs_scale=xg_sc[c][:], start=True, stop=True,
            )
            sums.append((e_ps, u_ps))

        def finish(c):
            e_ps, u_ps = sums[c]
            nc.scalar.activation(gate[c][:], e_ps, SILU)
            nc.vector.tensor_tensor(result[c][:], u_ps, gate[c][:], MULT)
            nc.sync.dma_start(out[:, starts[c] : starts[c] + CHUNKS[c]], result[c][:])

        for c in range(AHEAD):
            pick_third(c)
        for c in range(AHEAD):
            pick_fourth(c)
        multiply(0)
        pick_third(3)
        pick_fourth(3)
        multiply(1)
        pick_third(4)
        multiply(2)
        pick_fourth(4)
        finish(0)
        multiply(3)
        multiply(4)
        for c in range(1, len(CHUNKS)):
            finish(c)
